import numpy as np, ml_dtypes
CORES = [7,391,135,263,15,399,143,271]
N = 8
TK, NT = 128, 4
def setup_inputs(rng):
    x = rng.standard_normal((NT, 128, TK), dtype=np.float32).astype(ml_dtypes.bfloat16)
    return {"x": np.broadcast_to(x, (2, NT, 128, TK)).reshape(N, 128, TK).copy(), "w": rng.standard_normal((N, 128, NT * 128), dtype=np.float32).astype(ml_dtypes.bfloat16)}
def setup_inputs_big(rng):
    d = setup_inputs(rng)
    for k in ("x", "w"): d[k] = (d[k].astype(np.float32) * 1024.0).astype(d[k].dtype)
    return d
def setup_inputs_small(rng):
    d = setup_inputs(rng)
    for k in ("x", "w"): d[k] = (d[k].astype(np.float32) * (1 / 1024.0)).astype(d[k].dtype)
    return d
def setup_inputs_apart(rng):
    d = setup_inputs(rng)
    f = (10.0 ** rng.permutation(np.linspace(-1.5, 1.5, N))).astype(np.float32).reshape(N, 1, 1)
    for k in ("x", "w"): d[k] = (d[k].astype(np.float32) * f).astype(d[k].dtype)
    return d
def reference(x, w):
    X, W = x.astype(np.float64), w.astype(np.float64)
    y = np.stack([sum(W[r][:, 128 * j:128 * j + 128].T @ X[j if r < NT else j + NT] for j in range(NT)) for r in range(N)])
    return {"y": y.astype(ml_dtypes.bfloat16)}

SCRATCH = {
    "xd": ("dram", [128, 128], "bfloat16"),
    "rd": ("dram", [128, 128], "bfloat16"),
    "xs": ("sbuf", [128, 512], "bfloat16"),
    "wt": ("sbuf", [128, 512], "bfloat16"),
    "ys": ("sbuf", [128, 128], "bfloat16"),
    "acc": ("psum", [128, 128], "float32"),
}
SEMAPHORES = ["xd_in", "go", "own_in", "rd_in", "far_in", "near_in", "diag_in", "mm", "cp", "stored", "left"]


def _engines(mask):
    return [b for b in range(16) if (mask >> b) & 1]


def _mask_of(engines):
    m = 0
    for b in engines:
        m |= 1 << b
    return m


def rank_program(g, core, T, topo):
    rank = T.rank_of(core)
    if rank is None:
        return
    S = T.sem
    k = T.x.shape[1]
    nt = T.w.shape[1] // k

    def blk(c):
        j = T.rank_of(c) % nt
        return slice(j * k, (j + 1) * k)

    peers = [c for c in T.cores if c != core and topo.chip(c) == topo.chip(core)]
    near = [c for c in peers if topo.same_plane(core, c)][0]
    far = [c for c in peers if topo.may_write(core, c) and not topo.same_plane(core, c)][0]
    diag = [c for c in peers if not topo.may_write(core, c)][0]

    e_near = _engines(topo.mask(core, near))
    e_far = _engines(topo.mask(core, far))
    a1 = e_near[0::2]
    n_a1, n_far = len(a1), len(e_far)

    g.sync.dma_start(T.xd[:, :], T.x[:, :]).then_inc(S.xd_in, 16)
    g.sync.sem_inc(S.go, 1)
    g.sync.dma_start(T.xs[:, blk(core)], T.x[:, :]).then_inc(S.own_in, 16)
    g.scalar.wait_ge(S.go, 1)
    g.scalar.dma_start(T.wt[:, :], T.w[:, :]).then_inc(S.own_in, 16)

    rid_n, pid_n = topo.addr(near, core)
    rid_f, pid_f = topo.addr(far, core)
    g.wait_ge(S.xd_in, 16)
    g.remote_dma(out_ap=T.rd[:, :], in_ap=T.xd[:, :], remote_sem=S.rd_in, local_sem=S.left,
                 pid=pid_n, routing_id=rid_n, dma_engine_mask=_mask_of(a1))
    g.remote_dma(out_ap=T.xs[:, blk(core)], in_ap=T.xd[:, :], remote_sem=S.far_in, local_sem=S.left,
                 pid=pid_f, routing_id=rid_f, dma_engine_mask=_mask_of(e_far))
    g.wait_ge(S.rd_in, n_a1)
    g.remote_dma(out_ap=T.xs[:, blk(near)], in_ap=T.rd[:, :], remote_sem=S.diag_in, local_sem=S.left,
                 pid=pid_f, routing_id=rid_f, dma_engine_mask=_mask_of(e_far))

    g.sync.wait_ge(S.rd_in, n_a1)
    g.sync.dma_start(T.xs[:, blk(near)], T.rd[:, :]).then_inc(S.near_in, 16)

    te = g.tensor
    te.wait_ge(S.own_in, 32)
    te.matmul(T.acc[:, :], T.wt[:, blk(core)], T.xs[:, blk(core)], True, False)
    te.wait_ge(S.far_in, n_far)
    te.matmul(T.acc[:, :], T.wt[:, blk(far)], T.xs[:, blk(far)], False, False)
    te.wait_ge(S.near_in, 16)
    te.matmul(T.acc[:, :], T.wt[:, blk(near)], T.xs[:, blk(near)], False, False)
    te.wait_ge(S.diag_in, n_far)
    te.matmul(T.acc[:, :], T.wt[:, blk(diag)], T.xs[:, blk(diag)], False, True).then_inc(S.mm, 1)

    g.vector.wait_ge(S.mm, 1)
    g.vector.tensor_copy(T.ys[:, :], T.acc[:, :]).then_inc(S.cp, 1)

    g.sync.wait_ge(S.cp, 1)
    g.sync.dma_start(T.y[:, :], T.ys[:, :]).then_inc(S.stored, 16)
    g.sync.wait_ge(S.stored, 16)

    g.wait_ge(S.left, n_a1 + 2 * n_far)
